import numpy as np
import ml_dtypes


def mxq(x, axis, fmt="e4m3"):
    dtype, down = {"e4m3": (ml_dtypes.float8_e4m3fn, 7), "e5m2": (ml_dtypes.float8_e5m2, 14)}[fmt]
    v = np.moveaxis(np.asarray(x, np.float32).astype(ml_dtypes.bfloat16).astype(np.float64), axis, -1)
    blocks = v.reshape(v.shape[:-1] + (-1, 32))
    amax = np.abs(blocks).max(-1, keepdims=True)
    byte = np.maximum(np.where(amax > 0, np.frexp(amax)[1] - 1 + 127, 0) - down, 1)
    scale = np.exp2(byte - 127.0)
    codes = (blocks / scale).astype(np.float32).astype(dtype).astype(np.float64)
    return np.moveaxis((codes * scale).reshape(v.shape), -1, axis)


WIDE = False


def mx_kscale(k):
    if not WIDE:
        return np.ones(k)
    levels = np.array([18, -18])
    if k % 512:
        return np.exp2(np.random.permutation(np.resize(levels, k // 32))).repeat(32)
    a = np.empty((k // 512, 16))
    for p in range(k // 512):
        a[p, :8] = np.random.permutation(np.resize(levels, 8))
        for g in range(8):
            far = levels[np.abs(levels - a[p, g]) >= 10]
            a[p, g + 8] = far[np.random.randint(len(far))]
    return np.exp2(a.ravel()).repeat(32)


def f64(x):
    return np.asarray(x).astype(np.float64)


def striped(idx):
    return np.tile(np.asarray(idx).reshape(-1, 16).T, (8, 1)).astype(np.uint16)


def unstriped(offs):
    return offs[:16].T.reshape(-1).astype(np.int64)


E2M1 = np.array([0.0, 0.5, 1.0, 1.5, 2.0, 3.0, 4.0, 6.0, -0.0, -0.5, -1.0, -1.5, -2.0, -3.0, -4.0, -6.0])


def pack_weight(w, fmt):
    k, n = w.shape
    w = f64(np.asarray(w, np.float32).astype(ml_dtypes.bfloat16)).reshape(k // 32, 32, n)
    amax = np.abs(w).max(1)
    if fmt == "e4m3":
        byte = np.frexp(amax)[1] - 1 + 127 - 7
    else:
        mant, ex = np.frexp(amax / 6.0)
        byte = np.where(mant > 0.5, ex, ex - 1) + 127
    byte = np.clip(np.where(amax > 0, byte, 1), 1, 254)
    scaled = (w * np.exp2(127.0 - byte)[:, None, :]).reshape(k, n).astype(np.float32)
    by_word = np.ascontiguousarray(scaled.reshape(k // 512, 128, 4, n).transpose(0, 1, 3, 2))
    if fmt == "e4m3":
        words = by_word.astype(ml_dtypes.float8_e4m3fn).view(np.uint8)
    else:
        c = by_word.astype(ml_dtypes.float4_e2m1fn).view(np.uint8) & 0xF
        words = (c[..., 0::2] | (c[..., 1::2] << 4)).reshape(k // 512, 128, 2 * n)
    return np.ascontiguousarray(words), np.ascontiguousarray(byte.astype(np.uint8).reshape(k // 512, 16, n))


def unpack_weight(words, scales, fmt):
    g, _, n = scales.shape
    words = np.ascontiguousarray(words).reshape(g, 128, n, -1)
    if fmt == "e4m3":
        vals = words.view(ml_dtypes.float8_e4m3fn).astype(np.float64)
    else:
        nib = np.empty((g, 128, n, 4), np.uint8)
        nib[..., 0::2] = words & 0xF
        nib[..., 1::2] = words >> 4
        vals = E2M1[nib]
    vals = vals * np.repeat(np.exp2(scales.astype(np.float64) - 127.0), 8, axis=1)[..., None]
    return vals.transpose(0, 1, 3, 2).reshape(g * 512, n)


def planes(y):
    n, m = y.shape
    v = y.astype(np.float32).astype(ml_dtypes.bfloat16).astype(np.float64).reshape(n // 32, 32, m)
    top = np.abs(v).max(1)
    byte = np.clip(np.where(top > 0, np.frexp(top)[1] - 1 + 127 - 7, 1), 1, 254)
    codes = (v * np.exp2(127.0 - byte)[:, None, :]).reshape(n, m).astype(np.float32).astype(ml_dtypes.float8_e4m3fn).view(np.uint8)
    words = codes.reshape(n // 512, 128, 4, m).transpose(0, 1, 3, 2)
    return np.ascontiguousarray(words), np.ascontiguousarray(byte.astype(np.uint8).reshape(n // 512, 16, m))


def setup_inputs():
    n = np.random.standard_normal
    uni = np.random.uniform
    b0 = np.random.permutation(1024)
    b1 = np.random.permutation(1024)
    b2 = np.random.permutation(1024)
    f_e = mx_kscale(512)
    w0_ = pack_weight(n((512, 512)) / np.sqrt(512) / f_e[:, None], "e2m1")
    w1_ = pack_weight(n((512, 512)) / np.sqrt(512) / f_e[:, None], "e2m1")
    w2_ = pack_weight(n((512, 512)) / np.sqrt(512) / f_e[:, None], "e2m1")
    return {
        "dyT": (n((512, 1024)) * f_e[:, None]).astype(np.float32),
        "w0_words": w0_[0],
        "w0_scales": w0_[1],
        "w1_words": w1_[0],
        "w1_scales": w1_[1],
        "w2_words": w2_[0],
        "w2_scales": w2_[1],
        "b0offs": striped(b0),
        "b1offs": striped(b1),
        "b2offs": striped(b2),
    }


def reference(dyT, w0_words, w0_scales, w1_words, w1_scales, w2_words, w2_scales, b0offs, b1offs, b2offs):
    b0 = unstriped(b0offs)
    b1 = unstriped(b1offs)
    b2 = unstriped(b2offs)
    g0 = f64(dyT)[:, b0]
    g1 = f64(dyT)[:, b1]
    g2 = f64(dyT)[:, b2]
    w0 = unpack_weight(w0_words, w0_scales, "e2m1")
    x0 = w0.T @ mxq(g0, 0, "e5m2")
    w1 = unpack_weight(w1_words, w1_scales, "e2m1")
    x1 = w1.T @ mxq(g1, 0, "e5m2")
    w2 = unpack_weight(w2_words, w2_scales, "e2m1")
    x2 = w2.T @ mxq(g2, 0, "e5m2")
    out_0 = x0 + x1 + x2
    return (out_0,) + planes(out_0)

@@ -1,0 +1,233 @@
+from contextlib import ExitStack
+
+import concourse.mybir as mybir
+
+F32 = mybir.dt.float32
+BF16 = mybir.dt.bfloat16
+I32 = mybir.dt.int32
+U32 = mybir.dt.uint32
+U16 = mybir.dt.uint16
+U8 = mybir.dt.uint8
+E2M1X4 = mybir.dt.float4_e2m1fn_x4
+E5M2X4 = mybir.dt.float8_e5m2_x4
+E4M3X4 = mybir.dt.float8_e4m3fn_x4
+
+P = 128
+E = 512
+D = 512
+X = 1024
+TAPS = 3
+HALF = 512
+LANES = 4
+
+FLOPS = 2 * TAPS * E * D * X
+
+
+def tile_attend_gtap_x_pl_kernel(
+    tc, dyT, w0_words, w0_scales, w1_words, w1_scales, w2_words, w2_scales,
+    b0offs, b1offs, b2offs, out_0, out_1, out_2,
+):
+    nc = tc.nc
+    words_in = (w0_words, w1_words, w2_words)
+    scales_in = (w0_scales, w1_scales, w2_scales)
+    lists_in = (b0offs, b1offs, b2offs)
+    dy_rows = dyT.rearrange("(p a j) x -> p a j x", a=2, j=2)
+    out_rows = out_0.rearrange("(p t) x -> p t x", t=LANES)
+    out_words = out_1[0].rearrange("p x l -> p (x l)").bitcast(I32)
+    out_scales = out_2[0].bitcast(I32)
+
+    with ExitStack() as ctx:
+        keep = ctx.enter_context(tc.tile_pool(name="keep", bufs=1))
+        ring = ctx.enter_context(tc.tile_pool(name="ring", bufs=3))
+        psum = ctx.enter_context(tc.psum_pool(name="psum", bufs=1))
+
+        lists = [keep.tile([P, X // 16], U16, name="list%d" % k) for k in range(TAPS)]
+        chunks = ((0, 512, 832, X), (0, 512, X))
+        raw = [
+            [keep.tile([P, 2, hi - lo], F32, name="raw%d_%d" % (a, lo)) for lo, hi in zip(chunks[a], chunks[a][1:])]
+            for a in range(2)
+        ]
+        pairs = [keep.tile([P, 2 * X], BF16, name="pairs%d" % a, align_bytes=64) for a in range(2)]
+        w_raw = keep.tile([P, TAPS * 2 * D], U8, name="w_raw", align_bytes=64)
+        s_raw = keep.tile([P, D], U8, name="s_raw", align_bytes=64)
+        w_dealt = keep.tile([P, TAPS * 2 * D], U8, name="w_dealt", align_bytes=64)
+        s_dealt = [keep.tile([P, D], U8, name="s_dealt%d" % k, align_bytes=64) for k in range(TAPS)]
+        y_codes = keep.tile([P, X], U32, name="y_codes", align_bytes=64)
+        y_scales = keep.tile([P, X], U8, name="y_scales", align_bytes=64)
+
+        nc.gpsimd.memset(s_raw[:].bitcast(I32), 0)
+        for k in range(1, TAPS):
+            nc.gpsimd.memset(s_dealt[k][:].bitcast(I32), 0)
+
+        def load_dy(a, c):
+            nc.sync.dma_start(out=raw[a][c][:], in_=dy_rows[:, a, :, chunks[a][c]:chunks[a][c + 1]])
+
+        def load_scales(k):
+            for r in range(4):
+                nc.sync.dma_start(
+                    out=s_raw[32 * r + 4 * k:32 * r + 4 * k + 4, :].bitcast(I32),
+                    in_=scales_in[k][0][4 * r:4 * r + 4, :].bitcast(I32),
+                )
+
+        load_dy(0, 0)
+        nc.sync.dma_start(lists[0][:], lists_in[0])
+        load_dy(0, 1)
+        load_dy(0, 2)
+        nc.sync.dma_start(lists[1][:], lists_in[1])
+        load_dy(1, 0)
+        load_dy(1, 1)
+        nc.sync.dma_start(lists[2][:], lists_in[2])
+        for k in range(TAPS):
+            load_scales(k)
+        for k in range(TAPS):
+            nc.sync.dma_start(out=w_raw[:, 2 * D * k:2 * D * (k + 1)].bitcast(I32), in_=words_in[k][0].bitcast(I32))
+
+        def cast(a, c):
+            dst = pairs[a][:, 2 * chunks[a][c]:2 * chunks[a][c + 1]].rearrange("p (x j) -> p x j", j=2)
+            src = raw[a][c][:].rearrange("p j x -> p x j")
+            if a == 0:
+                nc.vector.tensor_copy(out=dst, in_=src)
+            else:
+                nc.scalar.copy(out=dst, in_=src)
+
+        for a in range(2):
+            for c in range(len(raw[a])):
+                cast(a, c)
+
+        def deal():
+            nc.vector.tensor_copy(
+                out=s_dealt[0][:].rearrange("p (t m) -> p t m", t=LANES),
+                in_=s_raw[:].rearrange("p (m t) -> p t m", t=LANES),
+            )
+            for k in range(1, TAPS):
+                nc.sync.dma_start(out=s_dealt[k][0:112, :].bitcast(I32), in_=s_dealt[0][4 * k:4 * k + 112, :].bitcast(I32))
+            nc.vector.tensor_copy(
+                out=w_dealt[:].bitcast(U16).rearrange("p (k t m) -> p k t m", k=TAPS, t=LANES),
+                in_=w_raw[:].bitcast(U16).rearrange("p (k m t) -> p k t m", k=TAPS, t=LANES),
+            )
+
+        acc = [[psum.tile([P, HALF], F32, name="acc%d%d" % (h, t)) for t in range(LANES)] for h in range(2)]
+        early = [keep.tile([P, 2 * HALF], U32, name="early%d" % k, align_bytes=64) for k in range(2)]
+        late = keep.tile([P, 5 * HALF], U32, name="late", align_bytes=64)
+        q = HALF // 2
+        pieces = [
+            (0, 0, 0, HALF, early[0], 0, HALF),
+            (0, 1, 0, HALF, early[1], 0, HALF),
+            (0, 2, 0, HALF, late, q, 2 * HALF + q),
+            (1, 0, 0, HALF, late, 0, HALF),
+            (1, 1, 0, HALF, late, 2 * HALF, 3 * HALF),
+            (1, 2, 0, q, late, 0, q),
+            (1, 2, q, q, late, 2 * HALF, 2 * HALF + q),
+        ]
+        woven = {}
+        codes = {}
+        scales = {}
+
+        def gather(u, a):
+            h, k, lo, width, held, first0, first1 = pieces[u]
+            first = (first0, first1)[a]
+            start = (h * HALF + lo) // 16
+            nc.vector.tensor_copy(
+                out=held[:, first:first + width],
+                in_=pairs[a][:].bitcast(U32).indirect(lists[k][:, start:start + width // 16]),
+            )
+
+        def weave(u, copy, word):
+            h, k, lo, width, held, first0, first1 = pieces[u]
+            if lo == 0:
+                woven[h, k] = ring.tile([P, LANES * HALF], BF16, name="woven", align_bytes=64)
+            step = first1 - first0
+            copy(
+                out=woven[h, k][:].bitcast(word)[:, 2 * lo:2 * (lo + width)].rearrange("p (x a) -> p x a", a=2),
+                in_=held[:, first0:first0 + 2 * step].bitcast(word).rearrange("p (a x) -> p x a", a=2)[:, 0:width, :],
+            )
+
+        def quantise(u):
+            h, k, lo, width, held, first0, first1 = pieces[u]
+            if lo == 0:
+                codes[h, k] = ring.tile([P, HALF], U32, name="codes", align_bytes=64)
+                scales[h, k] = ring.tile([P, HALF], U8, name="scales", align_bytes=64)
+            nc.vector.quantize_mx(
+                out=codes[h, k][:, lo:lo + width].bitcast(E5M2X4),
+                scales=scales[h, k][:, lo:lo + width],
+                in_=woven[h, k][:, LANES * lo:LANES * (lo + width)],
+            )
+
+        def multiply(h, k):
+            for t in range(LANES):
+                nc.tensor.matmul_mx(
+                    out=acc[h][t][:],
+                    lhsT=w_dealt[:, 2 * D * k + 2 * P * t:2 * D * k + 2 * P * (t + 1)].bitcast(E2M1X4),
+                    lhsT_scale=s_dealt[k][:, P * t:P * (t + 1)],
+                    rhs=codes[h, k][:].bitcast(E5M2X4),
+                    rhs_scale=scales[h, k][:],
+                    start=(k == 0),
+                    stop=(k == TAPS - 1),
+                )
+
+        y = [keep.tile([P, LANES, HALF], F32, name="y%d" % h, align_bytes=64) for h in range(2)]
+        y16 = [keep.tile([P, LANES * HALF], BF16, name="y16_%d" % h, align_bytes=64) for h in range(2)]
+
+        def drain(h, copies):
+            for t in range(LANES):
+                copies[t](out=y[h][:, t, :], in_=acc[h][t][:])
+                if t % 2 == 1:
+                    nc.sync.dma_start(
+                        out=out_rows[:, t - 1:t + 1, h * HALF:(h + 1) * HALF], in_=y[h][:, t - 1:t + 1, :]
+                    )
+
+        def interleave(h, lo, hi, copy):
+            copy(
+                out=y16[h][:, LANES * lo:LANES * hi].rearrange("p (c i t) -> p c t i", i=4, t=LANES),
+                in_=y[h][:, :, lo:hi].rearrange("p t (c i) -> p c t i", i=4),
+            )
+
+        def planes(h, lo, hi):
+            cols = slice(h * HALF + lo, h * HALF + hi)
+            nc.vector.quantize_mx(
+                out=y_codes[:, cols].bitcast(E4M3X4), scales=y_scales[:, cols], in_=y16[h][:, LANES * lo:LANES * hi]
+            )
+            nc.sync.dma_start(out=out_words[:, cols], in_=y_codes[:, cols].bitcast(I32))
+
+        on_scalar = nc.scalar.copy
+        on_vector = nc.vector.tensor_copy
+
+        for u in range(TAPS):
+            gather(u, 0)
+        deal()
+        for u in range(TAPS):
+            gather(u, 1)
+            weave(u, on_scalar, U32)
+            quantise(u)
+            multiply(0, u)
+        drain(0, [on_scalar] * LANES)
+        for u in (3, 4):
+            gather(u, 0)
+            gather(u, 1)
+        weave(3, on_scalar, U32)
+        quantise(3)
+        multiply(1, 0)
+        interleave(0, 0, q, on_scalar)
+        gather(5, 0)
+        gather(5, 1)
+        weave(4, on_scalar, U32)
+        quantise(4)
+        multiply(1, 1)
+        weave(5, on_scalar, U32)
+        gather(6, 0)
+        gather(6, 1)
+        quantise(5)
+        weave(6, on_vector, I32)
+        quantise(6)
+        multiply(1, 2)
+        interleave(0, q, HALF, on_scalar)
+        planes(0, 0, HALF)
+        drain(1, [on_scalar, on_vector] * 2)
+        interleave(1, 0, q, on_vector)
+        interleave(1, q, 336, on_vector)
+        interleave(1, 336, HALF, on_scalar)
+        planes(1, 0, q)
+        planes(1, q, HALF)
+        for r in range(4):
+            queue = nc.sync if r % 2 == 0 else nc.scalar
+            queue.dma_start(out=out_scales[4 * r:4 * r + 4, :], in_=y_scales[32 * r:32 * r + 4, :].bitcast(I32))

@@ -48,24 +48,26 @@ def tile_attend_gtap_x_pl_kernel(
             for a in range(2)
         ]
         pairs = [keep.tile([P, 2 * X], BF16, name="pairs%d" % a, align_bytes=64) for a in range(2)]
-        w_raw = keep.tile([P, TAPS * 2 * D], U8, name="w_raw", align_bytes=64)
-        s_raw = keep.tile([P, D], U8, name="s_raw", align_bytes=64)
-        w_dealt = keep.tile([P, TAPS * 2 * D], U8, name="w_dealt", align_bytes=64)
+        w_raw = [keep.tile([P, 2 * D], U8, name="w_raw", tag="after_w%d" % k, align_bytes=64) for k in range(TAPS)]
+        s_raw = [keep.tile([P, D], U8, name="s_raw", tag="after_s%d" % k, align_bytes=64) for k in range(TAPS)]
+        w_dealt = [keep.tile([P, 2 * D], U8, name="w_dealt%d" % k, align_bytes=64) for k in range(TAPS)]
         s_dealt = [keep.tile([P, D], U8, name="s_dealt%d" % k, align_bytes=64) for k in range(TAPS)]
         y_codes = keep.tile([P, X], U32, name="y_codes", align_bytes=64)
         y_scales = keep.tile([P, X], U8, name="y_scales", align_bytes=64)
 
-        nc.gpsimd.memset(s_raw[:].bitcast(I32), 0)
-        for k in range(1, TAPS):
-            nc.gpsimd.memset(s_dealt[k][:].bitcast(I32), 0)
+        for k in range(TAPS):
+            nc.gpsimd.memset(s_raw[k][:].bitcast(I32), 0)
 
         def load_dy(a, c):
             nc.sync.dma_start(out=raw[a][c][:], in_=dy_rows[:, a, :, chunks[a][c]:chunks[a][c + 1]])
 
-        def load_scales(k):
-            for r in range(4):
+        def load_words(k):
+            nc.sync.dma_start(out=w_raw[k][:].bitcast(I32), in_=words_in[k][0].bitcast(I32))
+
+        def load_scales(k, quadrants):
+            for r in quadrants:
                 nc.sync.dma_start(
-                    out=s_raw[32 * r + 4 * k:32 * r + 4 * k + 4, :].bitcast(I32),
+                    out=s_raw[k][32 * r:32 * r + 4, :].bitcast(I32),
                     in_=scales_in[k][0][4 * r:4 * r + 4, :].bitcast(I32),
                 )
 
@@ -75,12 +77,15 @@ def tile_attend_gtap_x_pl_kernel(
         load_dy(0, 2)
         nc.sync.dma_start(lists[1][:], lists_in[1])
         load_dy(1, 0)
+        load_scales(0, (0, 1))
         load_dy(1, 1)
+        load_scales(0, (2, 3))
+        load_words(0)
         nc.sync.dma_start(lists[2][:], lists_in[2])
-        for k in range(TAPS):
-            load_scales(k)
-        for k in range(TAPS):
-            nc.sync.dma_start(out=w_raw[:, 2 * D * k:2 * D * (k + 1)].bitcast(I32), in_=words_in[k][0].bitcast(I32))
+        load_scales(1, range(4))
+        load_words(1)
+        load_scales(2, range(4))
+        load_words(2)
 
         def cast(a, c):
             dst = pairs[a][:, 2 * chunks[a][c]:2 * chunks[a][c + 1]].rearrange("p (x j) -> p x j", j=2)
@@ -90,30 +95,34 @@ def tile_attend_gtap_x_pl_kernel(
             else:
                 nc.scalar.copy(out=dst, in_=src)
 
-        for a in range(2):
-            for c in range(len(raw[a])):
-                cast(a, c)
-
-        def deal():
-            nc.vector.tensor_copy(
-                out=s_dealt[0][:].rearrange("p (t m) -> p t m", t=LANES),
-                in_=s_raw[:].rearrange("p (m t) -> p t m", t=LANES),
+        rows16 = keep.tile([P, 2 * X], BF16, name="rows16", align_bytes=64)
+        for c in range(len(raw[0])):
+            cast(0, c)
+            nc.scalar.copy(
+                out=rows16[:].rearrange("p (j x) -> p j x", j=2)[:, :, chunks[0][c]:chunks[0][c + 1]], in_=raw[0][c][:]
             )
-            for k in range(1, TAPS):
-                nc.sync.dma_start(out=s_dealt[k][0:112, :].bitcast(I32), in_=s_dealt[0][4 * k:4 * k + 112, :].bitcast(I32))
+        for c in range(len(raw[1])):
+            cast(1, c)
+
+        def deal(k):
             nc.vector.tensor_copy(
-                out=w_dealt[:].bitcast(U16).rearrange("p (k t m) -> p k t m", k=TAPS, t=LANES),
-                in_=w_raw[:].bitcast(U16).rearrange("p (k m t) -> p k t m", k=TAPS, t=LANES),
+                out=w_dealt[k][:].bitcast(U16).rearrange("p (t m) -> p t m", t=LANES),
+                in_=w_raw[k][:].bitcast(U16).rearrange("p (m t) -> p t m", t=LANES),
+            )
+            nc.vector.tensor_copy(
+                out=s_dealt[k][:].rearrange("p (t m) -> p t m", t=LANES),
+                in_=s_raw[k][:].rearrange("p (m t) -> p t m", t=LANES),
             )
 
         acc = [[psum.tile([P, HALF], F32, name="acc%d%d" % (h, t)) for t in range(LANES)] for h in range(2)]
-        early = [keep.tile([P, 2 * HALF], U32, name="early%d" % k, align_bytes=64) for k in range(2)]
-        late = keep.tile([P, 5 * HALF], U32, name="late", align_bytes=64)
         q = HALF // 2
+        early = keep.tile([P, 3 * HALF], U32, name="early", align_bytes=64)
+        second = keep.tile([P, 2 * HALF], U32, name="second", tag="second", align_bytes=64)
+        late = keep.tile([P, 4 * HALF], U32, name="late", tag="second", align_bytes=64)
         pieces = [
-            (0, 0, 0, HALF, early[0], 0, HALF),
-            (0, 1, 0, HALF, early[1], 0, HALF),
-            (0, 2, 0, HALF, late, q, 2 * HALF + q),
+            (0, 0, 0, HALF, early, HALF, 2 * HALF),
+            (0, 1, 0, HALF, second, 0, HALF),
+            (0, 2, 0, HALF, early, 0, HALF),
             (1, 0, 0, HALF, late, 0, HALF),
             (1, 1, 0, HALF, late, 2 * HALF, 3 * HALF),
             (1, 2, 0, q, late, 0, q),
@@ -134,7 +143,13 @@ def tile_attend_gtap_x_pl_kernel(
 
         def weave(u, copy, word):
             h, k, lo, width, held, first0, first1 = pieces[u]
-            if lo == 0:
+            if (h, k) == (0, 2):
+                woven[h, k] = late[:, HALF + q:3 * HALF + q].bitcast(BF16)
+            elif (h, k) == (1, 1):
+                woven[h, k] = keep.tile([P, LANES * HALF], BF16, name="woven_turn", tag="after_w2", align_bytes=64)
+            elif (h, k, lo) == (1, 2, 0):
+                woven[h, k] = keep.tile([P, LANES * HALF], BF16, name="woven_last", tag="after_s2", align_bytes=64)
+            elif lo == 0:
                 woven[h, k] = ring.tile([P, LANES * HALF], BF16, name="woven", align_bytes=64)
             step = first1 - first0
             copy(
@@ -145,8 +160,12 @@ def tile_attend_gtap_x_pl_kernel(
         def quantise(u):
             h, k, lo, width, held, first0, first1 = pieces[u]
             if lo == 0:
-                codes[h, k] = ring.tile([P, HALF], U32, name="codes", align_bytes=64)
-                scales[h, k] = ring.tile([P, HALF], U8, name="scales", align_bytes=64)
+                if h == 0 and k > 0:
+                    codes[h, k] = keep.tile([P, HALF], U32, name="codes_turn", tag="after_s%d" % k, align_bytes=64)
+                    scales[h, k] = keep.tile([P, HALF], U8, name="scales_turn", tag="after_w%d" % k, align_bytes=64)
+                else:
+                    codes[h, k] = ring.tile([P, HALF], U32, name="codes", align_bytes=64)
+                    scales[h, k] = ring.tile([P, HALF], U8, name="scales", align_bytes=64)
             nc.vector.quantize_mx(
                 out=codes[h, k][:, lo:lo + width].bitcast(E5M2X4),
                 scales=scales[h, k][:, lo:lo + width],
@@ -157,7 +176,7 @@ def tile_attend_gtap_x_pl_kernel(
             for t in range(LANES):
                 nc.tensor.matmul_mx(
                     out=acc[h][t][:],
-                    lhsT=w_dealt[:, 2 * D * k + 2 * P * t:2 * D * k + 2 * P * (t + 1)].bitcast(E2M1X4),
+                    lhsT=w_dealt[k][:, 2 * P * t:2 * P * (t + 1)].bitcast(E2M1X4),
                     lhsT_scale=s_dealt[k][:, P * t:P * (t + 1)],
                     rhs=codes[h, k][:].bitcast(E5M2X4),
                     rhs_scale=scales[h, k][:],
@@ -168,8 +187,8 @@ def tile_attend_gtap_x_pl_kernel(
         y = [keep.tile([P, LANES, HALF], F32, name="y%d" % h, align_bytes=64) for h in range(2)]
         y16 = [keep.tile([P, LANES * HALF], BF16, name="y16_%d" % h, align_bytes=64) for h in range(2)]
 
-        def drain(h, copies):
-            for t in range(LANES):
+        def drain(h, copies, lanes):
+            for t in lanes:
                 copies[t](out=y[h][:, t, :], in_=acc[h][t][:])
                 if t % 2 == 1:
                     nc.sync.dma_start(
@@ -192,25 +211,43 @@ def tile_attend_gtap_x_pl_kernel(
         on_scalar = nc.scalar.copy
         on_vector = nc.vector.tensor_copy
 
+        def gather_row(j):
+            nc.scalar.activation(
+                out=late[:, 0:HALF].bitcast(BF16).rearrange("p (x j) -> p j x", j=2)[:, j, :],
+                in_=rows16[:, j * X:(j + 1) * X].indirect(lists[0][:, HALF // 16:X // 16]),
+                func=mybir.ActivationFunctionType.Copy,
+            )
+
         for u in range(TAPS):
             gather(u, 0)
-        deal()
-        for u in range(TAPS):
-            gather(u, 1)
-            weave(u, on_scalar, U32)
-            quantise(u)
-            multiply(0, u)
-        drain(0, [on_scalar] * LANES)
-        for u in (3, 4):
-            gather(u, 0)
-            gather(u, 1)
+        gather(0, 1)
+        gather(1, 1)
+        weave(0, on_scalar, U32)
+        deal(0)
+        quantise(0)
+        multiply(0, 0)
+        gather(2, 1)
+        weave(1, on_scalar, U32)
+        gather_row(0)
+        deal(1)
+        quantise(1)
+        multiply(0, 1)
+        weave(2, on_scalar, U32)
+        gather_row(1)
+        deal(2)
+        quantise(2)
+        multiply(0, 2)
+        gather(3, 1)
+        gather(4, 0)
+        gather(4, 1)
         weave(3, on_scalar, U32)
         quantise(3)
         multiply(1, 0)
-        interleave(0, 0, q, on_scalar)
         gather(5, 0)
         gather(5, 1)
+        drain(0, [on_scalar] * LANES, range(3))
         weave(4, on_scalar, U32)
+        drain(0, [on_scalar] * LANES, range(3, 4))
         quantise(4)
         multiply(1, 1)
         weave(5, on_scalar, U32)
@@ -220,12 +257,12 @@ def tile_attend_gtap_x_pl_kernel(
         weave(6, on_vector, I32)
         quantise(6)
         multiply(1, 2)
-        interleave(0, q, HALF, on_scalar)
+        interleave(0, 0, HALF, on_scalar)
         planes(0, 0, HALF)
-        drain(1, [on_scalar, on_vector] * 2)
+        drain(1, [on_scalar, on_vector] * 2, range(LANES))
         interleave(1, 0, q, on_vector)
-        interleave(1, q, 336, on_vector)
-        interleave(1, 336, HALF, on_scalar)
+        interleave(1, q, 384, on_vector)
+        interleave(1, 384, HALF, on_scalar)
         planes(1, 0, q)
         planes(1, q, HALF)
         for r in range(4):

@@ -39,19 +39,21 @@ def tile_attend_gtap_x_pl_kernel(
     with ExitStack() as ctx:
         keep = ctx.enter_context(tc.tile_pool(name="keep", bufs=1))
         ring = ctx.enter_context(tc.tile_pool(name="ring", bufs=3))
+        shared = ctx.enter_context(tc.tile_pool(name="shared", bufs=1))
         psum = ctx.enter_context(tc.psum_pool(name="psum", bufs=1))
 
         lists = [keep.tile([P, X // 16], U16, name="list%d" % k) for k in range(TAPS)]
         chunks = ((0, 512, 832, X), (0, 512, X))
         raw = [
-            [keep.tile([P, 2, hi - lo], F32, name="raw%d_%d" % (a, lo)) for lo, hi in zip(chunks[a], chunks[a][1:])]
+            [keep.tile([P, 2, hi - lo], F32, name="raw%d_%d" % (a, lo)) for lo, hi in zip(chunks[a], chunks[a][1:-a or None])]
             for a in range(2)
         ]
+        raw[1].append(shared.tile([P, 2, HALF], F32, name="raw_last", align_bytes=64, offset=0))
         pairs = [keep.tile([P, 2 * X], BF16, name="pairs%d" % a, align_bytes=64) for a in range(2)]
-        w_raw = [keep.tile([P, 2 * D], U8, name="w_raw", tag="after_w%d" % k, align_bytes=64) for k in range(TAPS)]
-        s_raw = [keep.tile([P, D], U8, name="s_raw", tag="after_s%d" % k, align_bytes=64) for k in range(TAPS)]
-        w_dealt = [keep.tile([P, 2 * D], U8, name="w_dealt%d" % k, align_bytes=64) for k in range(TAPS)]
-        s_dealt = [keep.tile([P, D], U8, name="s_dealt%d" % k, align_bytes=64) for k in range(TAPS)]
+        w_raw = [shared.tile([P, 2 * D], U8, name="w_raw%d" % k, align_bytes=64, offset=15360 - 1536 * k) for k in range(TAPS)]
+        s_raw = [shared.tile([P, D], U8, name="s_raw%d" % k, align_bytes=64, offset=16384 - 1536 * k) for k in range(TAPS)]
+        w_dealt = {}
+        s_dealt = {}
         y_codes = keep.tile([P, X], U32, name="y_codes", align_bytes=64)
         y_scales = keep.tile([P, X], U8, name="y_scales", align_bytes=64)
 
@@ -88,14 +90,14 @@ def tile_attend_gtap_x_pl_kernel(
         load_words(2)
 
         def cast(a, c):
-            dst = pairs[a][:, 2 * chunks[a][c]:2 * chunks[a][c + 1]].rearrange("p (x j) -> p x j", j=2)
-            src = raw[a][c][:].rearrange("p j x -> p x j")
+            dst = pairs[a][:, 2 * chunks[a][c]:2 * chunks[a][c + 1]].rearrange("p (c i j) -> p c j i", i=4, j=2)
+            src = raw[a][c][:].rearrange("p j (c i) -> p c j i", i=4)
             if a == 0:
                 nc.vector.tensor_copy(out=dst, in_=src)
             else:
                 nc.scalar.copy(out=dst, in_=src)
 
-        rows16 = keep.tile([P, 2 * X], BF16, name="rows16", align_bytes=64)
+        rows16 = shared.tile([P, 2 * X], BF16, name="rows16", align_bytes=64, offset=8192)
         for c in range(len(raw[0])):
             cast(0, c)
             nc.scalar.copy(
@@ -105,6 +107,12 @@ def tile_attend_gtap_x_pl_kernel(
             cast(1, c)
 
         def deal(k):
+            if k == 0:
+                w_dealt[k] = keep.tile([P, 2 * D], U8, name="w_dealt0", align_bytes=64)
+                s_dealt[k] = keep.tile([P, D], U8, name="s_dealt0", align_bytes=64)
+            else:
+                w_dealt[k] = shared.tile([P, 2 * D], U8, name="w_dealt%d" % k, align_bytes=64, offset=4096 * (k - 1))
+                s_dealt[k] = shared.tile([P, D], U8, name="s_dealt%d" % k, align_bytes=64, offset=4096 * (k - 1) + 1024)
             nc.vector.tensor_copy(
                 out=w_dealt[k][:].bitcast(U16).rearrange("p (t m) -> p t m", t=LANES),
                 in_=w_raw[k][:].bitcast(U16).rearrange("p (m t) -> p t m", t=LANES),
@@ -116,18 +124,19 @@ def tile_attend_gtap_x_pl_kernel(
 
         acc = [[psum.tile([P, HALF], F32, name="acc%d%d" % (h, t)) for t in range(LANES)] for h in range(2)]
         q = HALF // 2
-        early = keep.tile([P, 3 * HALF], U32, name="early", align_bytes=64)
-        second = keep.tile([P, 2 * HALF], U32, name="second", tag="second", align_bytes=64)
-        late = keep.tile([P, 4 * HALF], U32, name="late", tag="second", align_bytes=64)
+        early = keep.tile([P, 5 * HALF], U32, name="early", align_bytes=64)
+        late = shared.tile([P, 2 * HALF], U32, name="late", align_bytes=64, offset=11264)
         pieces = [
-            (0, 0, 0, HALF, early, HALF, 2 * HALF),
-            (0, 1, 0, HALF, second, 0, HALF),
-            (0, 2, 0, HALF, early, 0, HALF),
-            (1, 0, 0, HALF, late, 0, HALF),
-            (1, 1, 0, HALF, late, 2 * HALF, 3 * HALF),
-            (1, 2, 0, q, late, 0, q),
-            (1, 2, q, q, late, 2 * HALF, 2 * HALF + q),
+            (0, 0, 0, HALF, early, 3 * HALF, 4 * HALF),
+            (0, 1, 0, HALF, early, 0, HALF),
+            (0, 2, 0, HALF, early, 2 * HALF, 3 * HALF),
+            (1, 0, 0, HALF, early, HALF, 2 * HALF),
+            (1, 1, 0, HALF, late, 0, HALF),
+            (1, 2, 0, q, early, HALF, HALF + q),
+            (1, 2, q, q, late, 0, q),
         ]
+        turn = 24576
+        woven_at = {(0, 0): 4096, (1, 1): turn + 1536, (1, 2): turn + 5632}
         woven = {}
         codes = {}
         scales = {}
@@ -143,26 +152,26 @@ def tile_attend_gtap_x_pl_kernel(
 
         def weave(u, copy, word):
             h, k, lo, width, held, first0, first1 = pieces[u]
-            if (h, k) == (0, 2):
-                woven[h, k] = late[:, HALF + q:3 * HALF + q].bitcast(BF16)
-            elif (h, k) == (1, 1):
-                woven[h, k] = keep.tile([P, LANES * HALF], BF16, name="woven_turn", tag="after_w2", align_bytes=64)
-            elif (h, k, lo) == (1, 2, 0):
-                woven[h, k] = keep.tile([P, LANES * HALF], BF16, name="woven_last", tag="after_s2", align_bytes=64)
+            if lo == 0 and (h, k) in woven_at:
+                woven[h, k] = shared.tile(
+                    [P, LANES * HALF], BF16, name="woven%d%d" % (h, k), align_bytes=64, offset=woven_at[h, k]
+                )
             elif lo == 0:
                 woven[h, k] = ring.tile([P, LANES * HALF], BF16, name="woven", align_bytes=64)
             step = first1 - first0
             copy(
-                out=woven[h, k][:].bitcast(word)[:, 2 * lo:2 * (lo + width)].rearrange("p (x a) -> p x a", a=2),
-                in_=held[:, first0:first0 + 2 * step].bitcast(word).rearrange("p (a x) -> p x a", a=2)[:, 0:width, :],
+                out=woven[h, k][:].bitcast(word)[:, 2 * lo:2 * (lo + width)].rearrange("p (c i a) -> p c a i", i=4, a=2),
+                in_=held[:, first0:first0 + 2 * step].bitcast(word).rearrange("p (a c i) -> p c a i", a=2, i=4)[
+                    :, 0:width // 4, :, :
+                ],
             )
 
         def quantise(u):
             h, k, lo, width, held, first0, first1 = pieces[u]
             if lo == 0:
-                if h == 0 and k > 0:
-                    codes[h, k] = keep.tile([P, HALF], U32, name="codes_turn", tag="after_s%d" % k, align_bytes=64)
-                    scales[h, k] = keep.tile([P, HALF], U8, name="scales_turn", tag="after_w%d" % k, align_bytes=64)
+                if (h, k) == (0, 2):
+                    codes[h, k] = shared.tile([P, HALF], U32, name="codes_turn", align_bytes=64, offset=turn)
+                    scales[h, k] = shared.tile([P, HALF], U8, name="scales_turn", align_bytes=64, offset=turn + 6144)
                 else:
                     codes[h, k] = ring.tile([P, HALF], U32, name="codes", align_bytes=64)
                     scales[h, k] = ring.tile([P, HALF], U8, name="scales", align_bytes=64)
@@ -213,39 +222,39 @@ def tile_attend_gtap_x_pl_kernel(
 
         def gather_row(j):
             nc.scalar.activation(
-                out=late[:, 0:HALF].bitcast(BF16).rearrange("p (x j) -> p j x", j=2)[:, j, :],
+                out=early[:, HALF:2 * HALF].bitcast(BF16).rearrange("p (x j) -> p j x", j=2)[:, j, :],
                 in_=rows16[:, j * X:(j + 1) * X].indirect(lists[0][:, HALF // 16:X // 16]),
                 func=mybir.ActivationFunctionType.Copy,
             )
 
         for u in range(TAPS):
             gather(u, 0)
+        deal(0)
         gather(0, 1)
         gather(1, 1)
+        deal(1)
         weave(0, on_scalar, U32)
-        deal(0)
         quantise(0)
         multiply(0, 0)
         gather(2, 1)
+        deal(2)
         weave(1, on_scalar, U32)
         gather_row(0)
-        deal(1)
         quantise(1)
         multiply(0, 1)
         weave(2, on_scalar, U32)
         gather_row(1)
-        deal(2)
         quantise(2)
         multiply(0, 2)
         gather(3, 1)
         gather(4, 0)
         gather(4, 1)
         weave(3, on_scalar, U32)
+        drain(0, [on_scalar] * LANES, range(3))
         quantise(3)
         multiply(1, 0)
         gather(5, 0)
         gather(5, 1)
-        drain(0, [on_scalar] * LANES, range(3))
         weave(4, on_scalar, U32)
         drain(0, [on_scalar] * LANES, range(3, 4))
         quantise(4)

@@ -17,8 +17,25 @@ E = 512
 D = 512
 X = 1024
 TAPS = 3
-HALF = 512
 LANES = 4
+HALF = 512
+QUARTER = HALF // 2
+ENTRIES = 16
+RUN = 4
+KIB = 1024
+
+CHUNKS = ((0, 512, 832, X), (0, 512, X))
+VECTOR_COLUMNS = 384
+
+W_RAW_AT = (20 * KIB, 4 * KIB, 6 * KIB)
+S_RAW_AT = (21 * KIB, 5 * KIB, 5 * KIB + 512)
+CODES2_AT = 4 * KIB + 512
+SCALES2_AT = 10 * KIB
+WOVEN3_AT = 1 * KIB
+WOVEN4_AT = 6 * KIB
+WOVEN2_HIGH_AT = 14 * KIB
+PICKED4_AT = 14 * KIB
+WOVEN5_AT = 14 * KIB
 
 FLOPS = 2 * TAPS * E * D * X
 
@@ -35,6 +52,8 @@ def tile_attend_gtap_x_pl_kernel(
     out_rows = out_0.rearrange("(p t) x -> p t x", t=LANES)
     out_words = out_1[0].rearrange("p x l -> p (x l)").bitcast(I32)
     out_scales = out_2[0].bitcast(I32)
+    on_scalar = nc.scalar.copy
+    on_vector = nc.vector.tensor_copy
 
     with ExitStack() as ctx:
         keep = ctx.enter_context(tc.tile_pool(name="keep", bufs=1))
@@ -42,18 +61,18 @@ def tile_attend_gtap_x_pl_kernel(
         shared = ctx.enter_context(tc.tile_pool(name="shared", bufs=1))
         psum = ctx.enter_context(tc.psum_pool(name="psum", bufs=1))
 
-        lists = [keep.tile([P, X // 16], U16, name="list%d" % k) for k in range(TAPS)]
-        chunks = ((0, 512, 832, X), (0, 512, X))
+        lists = [keep.tile([P, X // ENTRIES], U16, name="list%d" % k) for k in range(TAPS)]
         raw = [
-            [keep.tile([P, 2, hi - lo], F32, name="raw%d_%d" % (a, lo)) for lo, hi in zip(chunks[a], chunks[a][1:-a or None])]
+            [keep.tile([P, 2, hi - lo], F32, name="raw%d_%d" % (a, lo)) for lo, hi in zip(CHUNKS[a], CHUNKS[a][1:])]
             for a in range(2)
         ]
-        raw[1].append(shared.tile([P, 2, HALF], F32, name="raw_last", align_bytes=64, offset=0))
         pairs = [keep.tile([P, 2 * X], BF16, name="pairs%d" % a, align_bytes=64) for a in range(2)]
-        w_raw = [shared.tile([P, 2 * D], U8, name="w_raw%d" % k, align_bytes=64, offset=15360 - 1536 * k) for k in range(TAPS)]
-        s_raw = [shared.tile([P, D], U8, name="s_raw%d" % k, align_bytes=64, offset=16384 - 1536 * k) for k in range(TAPS)]
-        w_dealt = {}
-        s_dealt = {}
+        w_raw = [
+            shared.tile([P, 2 * D], U8, name="w_raw%d" % k, align_bytes=64, offset=W_RAW_AT[k]) for k in range(TAPS)
+        ]
+        s_raw = [shared.tile([P, D], U8, name="s_raw%d" % k, align_bytes=64, offset=S_RAW_AT[k]) for k in range(TAPS)]
+        w_dealt = [keep.tile([P, 2 * D], U8, name="w_dealt%d" % k, align_bytes=64) for k in range(TAPS)]
+        s_dealt = [keep.tile([P, D], U8, name="s_dealt%d" % k, align_bytes=64) for k in range(TAPS)]
         y_codes = keep.tile([P, X], U32, name="y_codes", align_bytes=64)
         y_scales = keep.tile([P, X], U8, name="y_scales", align_bytes=64)
 
@@ -61,7 +80,10 @@ def tile_attend_gtap_x_pl_kernel(
             nc.gpsimd.memset(s_raw[k][:].bitcast(I32), 0)
 
         def load_dy(a, c):
-            nc.sync.dma_start(out=raw[a][c][:], in_=dy_rows[:, a, :, chunks[a][c]:chunks[a][c + 1]])
+            nc.sync.dma_start(out=raw[a][c][:], in_=dy_rows[:, a, :, CHUNKS[a][c]:CHUNKS[a][c + 1]])
+
+        def load_list(k):
+            nc.sync.dma_start(lists[k][:], lists_in[k])
 
         def load_words(k):
             nc.sync.dma_start(out=w_raw[k][:].bitcast(I32), in_=words_in[k][0].bitcast(I32))
@@ -74,45 +96,37 @@ def tile_attend_gtap_x_pl_kernel(
                 )
 
         load_dy(0, 0)
-        nc.sync.dma_start(lists[0][:], lists_in[0])
+        load_list(0)
         load_dy(0, 1)
         load_dy(0, 2)
-        nc.sync.dma_start(lists[1][:], lists_in[1])
+        load_list(1)
         load_dy(1, 0)
         load_scales(0, (0, 1))
         load_dy(1, 1)
         load_scales(0, (2, 3))
         load_words(0)
-        nc.sync.dma_start(lists[2][:], lists_in[2])
+        load_list(2)
         load_scales(1, range(4))
         load_words(1)
         load_scales(2, range(4))
         load_words(2)
 
-        def cast(a, c):
-            dst = pairs[a][:, 2 * chunks[a][c]:2 * chunks[a][c + 1]].rearrange("p (c i j) -> p c j i", i=4, j=2)
-            src = raw[a][c][:].rearrange("p j (c i) -> p c j i", i=4)
-            if a == 0:
-                nc.vector.tensor_copy(out=dst, in_=src)
-            else:
-                nc.scalar.copy(out=dst, in_=src)
+        def cast_pairs(a, c, copy):
+            copy(
+                out=pairs[a][:, 2 * CHUNKS[a][c]:2 * CHUNKS[a][c + 1]].rearrange("p (c i j) -> p c j i", i=RUN, j=2),
+                in_=raw[a][c][:].rearrange("p j (c i) -> p c j i", i=RUN),
+            )
 
-        rows16 = shared.tile([P, 2 * X], BF16, name="rows16", align_bytes=64, offset=8192)
+        rows16 = keep.tile([P, 2 * X], BF16, name="rows16", align_bytes=64)
         for c in range(len(raw[0])):
-            cast(0, c)
+            cast_pairs(0, c, on_vector)
             nc.scalar.copy(
-                out=rows16[:].rearrange("p (j x) -> p j x", j=2)[:, :, chunks[0][c]:chunks[0][c + 1]], in_=raw[0][c][:]
+                out=rows16[:].rearrange("p (j x) -> p j x", j=2)[:, :, CHUNKS[0][c]:CHUNKS[0][c + 1]], in_=raw[0][c][:]
             )
         for c in range(len(raw[1])):
-            cast(1, c)
+            cast_pairs(1, c, on_scalar)
 
         def deal(k):
-            if k == 0:
-                w_dealt[k] = keep.tile([P, 2 * D], U8, name="w_dealt0", align_bytes=64)
-                s_dealt[k] = keep.tile([P, D], U8, name="s_dealt0", align_bytes=64)
-            else:
-                w_dealt[k] = shared.tile([P, 2 * D], U8, name="w_dealt%d" % k, align_bytes=64, offset=4096 * (k - 1))
-                s_dealt[k] = shared.tile([P, D], U8, name="s_dealt%d" % k, align_bytes=64, offset=4096 * (k - 1) + 1024)
             nc.vector.tensor_copy(
                 out=w_dealt[k][:].bitcast(U16).rearrange("p (t m) -> p t m", t=LANES),
                 in_=w_raw[k][:].bitcast(U16).rearrange("p (m t) -> p t m", t=LANES),
@@ -123,72 +137,67 @@ def tile_attend_gtap_x_pl_kernel(
             )
 
         acc = [[psum.tile([P, HALF], F32, name="acc%d%d" % (h, t)) for t in range(LANES)] for h in range(2)]
-        q = HALF // 2
-        early = keep.tile([P, 5 * HALF], U32, name="early", align_bytes=64)
-        late = shared.tile([P, 2 * HALF], U32, name="late", align_bytes=64, offset=11264)
-        pieces = [
-            (0, 0, 0, HALF, early, 3 * HALF, 4 * HALF),
-            (0, 1, 0, HALF, early, 0, HALF),
-            (0, 2, 0, HALF, early, 2 * HALF, 3 * HALF),
-            (1, 0, 0, HALF, early, HALF, 2 * HALF),
-            (1, 1, 0, HALF, late, 0, HALF),
-            (1, 2, 0, q, early, HALF, HALF + q),
-            (1, 2, q, q, late, 0, q),
+
+        picked02 = keep.tile([P, 3 * HALF], U32, name="picked02", align_bytes=64)
+        picked1 = keep.tile([P, 2 * HALF], U32, name="picked1", tag="picked135", align_bytes=64)
+        picked35 = keep.tile([P, 2 * HALF], U32, name="picked35", tag="picked135", align_bytes=64)
+        woven2_high = shared.tile([P, LANES * QUARTER], BF16, name="woven2_high", align_bytes=64, offset=WOVEN2_HIGH_AT)
+        picked4 = shared.tile([P, 2 * HALF], U32, name="picked4", align_bytes=64, offset=PICKED4_AT)
+        picked = [
+            picked02[:, HALF:3 * HALF], picked1[:], picked02[:, 0:2 * HALF], picked35[:], picked4[:], picked35[:]
         ]
-        turn = 24576
-        woven_at = {(0, 0): 4096, (1, 1): turn + 1536, (1, 2): turn + 5632}
+        woven2_low = picked35[:, HALF:2 * HALF].bitcast(BF16)
         woven = {}
         codes = {}
         scales = {}
 
+        def entries(u):
+            h, k = divmod(u, TAPS)
+            return lists[k][:, h * HALF // ENTRIES:(h + 1) * HALF // ENTRIES]
+
         def gather(u, a):
-            h, k, lo, width, held, first0, first1 = pieces[u]
-            first = (first0, first1)[a]
-            start = (h * HALF + lo) // 16
             nc.vector.tensor_copy(
-                out=held[:, first:first + width],
-                in_=pairs[a][:].bitcast(U32).indirect(lists[k][:, start:start + width // 16]),
+                out=picked[u][:, a * HALF:(a + 1) * HALF], in_=pairs[a][:].bitcast(U32).indirect(entries(u))
             )
 
-        def weave(u, copy, word):
-            h, k, lo, width, held, first0, first1 = pieces[u]
-            if lo == 0 and (h, k) in woven_at:
-                woven[h, k] = shared.tile(
-                    [P, LANES * HALF], BF16, name="woven%d%d" % (h, k), align_bytes=64, offset=woven_at[h, k]
-                )
-            elif lo == 0:
-                woven[h, k] = ring.tile([P, LANES * HALF], BF16, name="woven", align_bytes=64)
-            step = first1 - first0
-            copy(
-                out=woven[h, k][:].bitcast(word)[:, 2 * lo:2 * (lo + width)].rearrange("p (c i a) -> p c a i", i=4, a=2),
-                in_=held[:, first0:first0 + 2 * step].bitcast(word).rearrange("p (a c i) -> p c a i", a=2, i=4)[
-                    :, 0:width // 4, :, :
-                ],
+        def gather_row(u, j):
+            nc.scalar.activation(
+                out=picked[u][:, 0:HALF].bitcast(BF16).rearrange("p (x j) -> p j x", j=2)[:, j, :],
+                in_=rows16[:, j * X:(j + 1) * X].indirect(entries(u)),
+                func=mybir.ActivationFunctionType.Copy,
             )
+
+        def weave(dst, u, lo, hi, copy, word):
+            copy(
+                out=dst.bitcast(word).rearrange("p (c i a) -> p c a i", i=RUN, a=2),
+                in_=picked[u].bitcast(word).rearrange("p (a c i) -> p c a i", a=2, i=RUN)[:, lo // RUN:hi // RUN, :, :],
+            )
+
+        def weave_first_half(u):
+            woven[u] = ring.tile([P, LANES * HALF], BF16, name="woven", align_bytes=64)
+            weave(woven[u][:], u, 0, HALF, on_scalar, U32)
+
+        def weave_second_half(u, offset, copy, word):
+            woven[u] = shared.tile([P, LANES * HALF], BF16, name="woven%d" % u, align_bytes=64, offset=offset)
+            weave(woven[u][:], u, 0, HALF, copy, word)
+
+        def quantise_columns(u, lo, hi, src):
+            nc.vector.quantize_mx(out=codes[u][:, lo:hi].bitcast(E5M2X4), scales=scales[u][:, lo:hi], in_=src)
 
         def quantise(u):
-            h, k, lo, width, held, first0, first1 = pieces[u]
-            if lo == 0:
-                if (h, k) == (0, 2):
-                    codes[h, k] = shared.tile([P, HALF], U32, name="codes_turn", align_bytes=64, offset=turn)
-                    scales[h, k] = shared.tile([P, HALF], U8, name="scales_turn", align_bytes=64, offset=turn + 6144)
-                else:
-                    codes[h, k] = ring.tile([P, HALF], U32, name="codes", align_bytes=64)
-                    scales[h, k] = ring.tile([P, HALF], U8, name="scales", align_bytes=64)
-            nc.vector.quantize_mx(
-                out=codes[h, k][:, lo:lo + width].bitcast(E5M2X4),
-                scales=scales[h, k][:, lo:lo + width],
-                in_=woven[h, k][:, LANES * lo:LANES * (lo + width)],
-            )
+            codes[u] = ring.tile([P, HALF], U32, name="codes", align_bytes=64)
+            scales[u] = ring.tile([P, HALF], U8, name="scales", align_bytes=64)
+            quantise_columns(u, 0, HALF, woven[u][:])
 
-        def multiply(h, k):
+        def multiply(u):
+            h, k = divmod(u, TAPS)
             for t in range(LANES):
                 nc.tensor.matmul_mx(
                     out=acc[h][t][:],
                     lhsT=w_dealt[k][:, 2 * P * t:2 * P * (t + 1)].bitcast(E2M1X4),
                     lhsT_scale=s_dealt[k][:, P * t:P * (t + 1)],
-                    rhs=codes[h, k][:].bitcast(E5M2X4),
-                    rhs_scale=scales[h, k][:],
+                    rhs=codes[u][:].bitcast(E5M2X4),
+                    rhs_scale=scales[u][:],
                     start=(k == 0),
                     stop=(k == TAPS - 1),
                 )
@@ -196,18 +205,15 @@ def tile_attend_gtap_x_pl_kernel(
         y = [keep.tile([P, LANES, HALF], F32, name="y%d" % h, align_bytes=64) for h in range(2)]
         y16 = [keep.tile([P, LANES * HALF], BF16, name="y16_%d" % h, align_bytes=64) for h in range(2)]
 
-        def drain(h, copies, lanes):
-            for t in lanes:
-                copies[t](out=y[h][:, t, :], in_=acc[h][t][:])
-                if t % 2 == 1:
-                    nc.sync.dma_start(
-                        out=out_rows[:, t - 1:t + 1, h * HALF:(h + 1) * HALF], in_=y[h][:, t - 1:t + 1, :]
-                    )
+        def empty_bank(h, t, copy):
+            copy(out=y[h][:, t, :], in_=acc[h][t][:])
+            if t % 2 == 1:
+                nc.sync.dma_start(out=out_rows[:, t - 1:t + 1, h * HALF:(h + 1) * HALF], in_=y[h][:, t - 1:t + 1, :])
 
-        def interleave(h, lo, hi, copy):
+        def round_result(h, lo, hi, copy):
             copy(
-                out=y16[h][:, LANES * lo:LANES * hi].rearrange("p (c i t) -> p c t i", i=4, t=LANES),
-                in_=y[h][:, :, lo:hi].rearrange("p t (c i) -> p c t i", i=4),
+                out=y16[h][:, LANES * lo:LANES * hi].rearrange("p (c i t) -> p c t i", i=RUN, t=LANES),
+                in_=y[h][:, :, lo:hi].rearrange("p t (c i) -> p c t i", i=RUN),
             )
 
         def planes(h, lo, hi):
@@ -217,63 +223,57 @@ def tile_attend_gtap_x_pl_kernel(
             )
             nc.sync.dma_start(out=out_words[:, cols], in_=y_codes[:, cols].bitcast(I32))
 
-        on_scalar = nc.scalar.copy
-        on_vector = nc.vector.tensor_copy
-
-        def gather_row(j):
-            nc.scalar.activation(
-                out=early[:, HALF:2 * HALF].bitcast(BF16).rearrange("p (x j) -> p j x", j=2)[:, j, :],
-                in_=rows16[:, j * X:(j + 1) * X].indirect(lists[0][:, HALF // 16:X // 16]),
-                func=mybir.ActivationFunctionType.Copy,
-            )
-
         for u in range(TAPS):
             gather(u, 0)
         deal(0)
         gather(0, 1)
         gather(1, 1)
-        deal(1)
-        weave(0, on_scalar, U32)
+        weave_first_half(0)
         quantise(0)
-        multiply(0, 0)
+        multiply(0)
         gather(2, 1)
-        deal(2)
-        weave(1, on_scalar, U32)
-        gather_row(0)
+        weave_first_half(1)
+        gather_row(3, 0)
         quantise(1)
-        multiply(0, 1)
-        weave(2, on_scalar, U32)
-        gather_row(1)
-        quantise(2)
-        multiply(0, 2)
+        deal(1)
+        multiply(1)
+        deal(2)
+        weave(woven2_low, 2, 0, QUARTER, on_scalar, U32)
+        weave(woven2_high[:], 2, QUARTER, HALF, on_scalar, U32)
+        gather_row(3, 1)
+        codes[2] = shared.tile([P, HALF], U32, name="codes2", align_bytes=64, offset=CODES2_AT)
+        scales[2] = shared.tile([P, HALF], U8, name="scales2", align_bytes=64, offset=SCALES2_AT)
+        quantise_columns(2, 0, QUARTER, woven2_low)
+        quantise_columns(2, QUARTER, HALF, woven2_high[:])
+        multiply(2)
+
         gather(3, 1)
         gather(4, 0)
         gather(4, 1)
-        weave(3, on_scalar, U32)
-        drain(0, [on_scalar] * LANES, range(3))
+        for t in range(LANES - 1):
+            empty_bank(0, t, on_scalar)
+        weave_second_half(3, WOVEN3_AT, on_scalar, U32)
+        weave_second_half(4, WOVEN4_AT, on_scalar, U32)
+        empty_bank(0, LANES - 1, on_scalar)
         quantise(3)
-        multiply(1, 0)
+        multiply(3)
         gather(5, 0)
         gather(5, 1)
-        weave(4, on_scalar, U32)
-        drain(0, [on_scalar] * LANES, range(3, 4))
         quantise(4)
-        multiply(1, 1)
-        weave(5, on_scalar, U32)
-        gather(6, 0)
-        gather(6, 1)
+        multiply(4)
+        weave_second_half(5, WOVEN5_AT, on_vector, I32)
         quantise(5)
-        weave(6, on_vector, I32)
-        quantise(6)
-        multiply(1, 2)
-        interleave(0, 0, HALF, on_scalar)
+        multiply(5)
+        round_result(0, 0, HALF, on_scalar)
         planes(0, 0, HALF)
-        drain(1, [on_scalar, on_vector] * 2, range(LANES))
-        interleave(1, 0, q, on_vector)
-        interleave(1, q, 384, on_vector)
-        interleave(1, 384, HALF, on_scalar)
-        planes(1, 0, q)
-        planes(1, q, HALF)
+
+        for t in range(LANES):
+            empty_bank(1, t, on_scalar if t % 2 == 0 else on_vector)
+        round_result(1, 0, QUARTER, on_vector)
+        round_result(1, QUARTER, VECTOR_COLUMNS, on_vector)
+        round_result(1, VECTOR_COLUMNS, HALF, on_scalar)
+        planes(1, 0, QUARTER)
+        planes(1, QUARTER, HALF)
         for r in range(4):
             queue = nc.sync if r % 2 == 0 else nc.scalar
             queue.dma_start(out=out_scales[4 * r:4 * r + 4, :], in_=y_scales[32 * r:32 * r + 4, :].bitcast(I32))

@@ -100,12 +100,12 @@ def tile_attend_gtap_x_pl_kernel(
         load_dy(0, 1)
         load_dy(0, 2)
         load_list(1)
-        load_dy(1, 0)
-        load_scales(0, (0, 1))
-        load_dy(1, 1)
-        load_scales(0, (2, 3))
-        load_words(0)
         load_list(2)
+        load_dy(1, 0)
+        load_scales(0, range(1))
+        load_dy(1, 1)
+        load_scales(0, range(1, 4))
+        load_words(0)
         load_scales(1, range(4))
         load_words(1)
         load_scales(2, range(4))

from contextlib import ExitStack

import concourse.mybir as mybir

F32 = mybir.dt.float32
BF16 = mybir.dt.bfloat16
I32 = mybir.dt.int32
U32 = mybir.dt.uint32
U16 = mybir.dt.uint16
U8 = mybir.dt.uint8
E2M1X4 = mybir.dt.float4_e2m1fn_x4
E5M2X4 = mybir.dt.float8_e5m2_x4
E4M3X4 = mybir.dt.float8_e4m3fn_x4

P = 128
E = 512
D = 512
X = 1024
TAPS = 3
LANES = 4
HALF = 512
QUARTER = HALF // 2
ENTRIES = 16
RUN = 4
KIB = 1024

CHUNKS = ((0, 512, 832, X), (0, 512, X))
VECTOR_COLUMNS = 384

W_RAW_AT = (20 * KIB, 4 * KIB, 6 * KIB)
S_RAW_AT = (21 * KIB, 5 * KIB, 5 * KIB + 512)
CODES2_AT = 4 * KIB + 512
SCALES2_AT = 10 * KIB
WOVEN3_AT = 1 * KIB
WOVEN4_AT = 6 * KIB
WOVEN2_HIGH_AT = 14 * KIB
PICKED4_AT = 14 * KIB
WOVEN5_AT = 14 * KIB

FLOPS = 2 * TAPS * E * D * X


def tile_attend_gtap_x_pl_kernel(
    tc, dyT, w0_words, w0_scales, w1_words, w1_scales, w2_words, w2_scales,
    b0offs, b1offs, b2offs, out_0, out_1, out_2,
):
    nc = tc.nc
    words_in = (w0_words, w1_words, w2_words)
    scales_in = (w0_scales, w1_scales, w2_scales)
    lists_in = (b0offs, b1offs, b2offs)
    dy_rows = dyT.rearrange("(p a j) x -> p a j x", a=2, j=2)
    out_rows = out_0.rearrange("(p t) x -> p t x", t=LANES)
    out_words = out_1[0].rearrange("p x l -> p (x l)").bitcast(I32)
    out_scales = out_2[0].bitcast(I32)
    on_scalar = nc.scalar.copy
    on_vector = nc.vector.tensor_copy

    with ExitStack() as ctx:
        keep = ctx.enter_context(tc.tile_pool(name="keep", bufs=1))
        ring = ctx.enter_context(tc.tile_pool(name="ring", bufs=3))
        shared = ctx.enter_context(tc.tile_pool(name="shared", bufs=1))
        psum = ctx.enter_context(tc.psum_pool(name="psum", bufs=1))

        lists = [keep.tile([P, X // ENTRIES], U16, name="list%d" % k) for k in range(TAPS)]
        raw = [
            [keep.tile([P, 2, hi - lo], F32, name="raw%d_%d" % (a, lo)) for lo, hi in zip(CHUNKS[a], CHUNKS[a][1:])]
            for a in range(2)
        ]
        pairs = [keep.tile([P, 2 * X], BF16, name="pairs%d" % a, align_bytes=64) for a in range(2)]
        w_raw = [
            shared.tile([P, 2 * D], U8, name="w_raw%d" % k, align_bytes=64, offset=W_RAW_AT[k]) for k in range(TAPS)
        ]
        s_raw = [shared.tile([P, D], U8, name="s_raw%d" % k, align_bytes=64, offset=S_RAW_AT[k]) for k in range(TAPS)]
        w_dealt = [keep.tile([P, 2 * D], U8, name="w_dealt%d" % k, align_bytes=64) for k in range(TAPS)]
        s_dealt = [keep.tile([P, D], U8, name="s_dealt%d" % k, align_bytes=64) for k in range(TAPS)]
        y_codes = keep.tile([P, X], U32, name="y_codes", align_bytes=64)
        y_scales = keep.tile([P, X], U8, name="y_scales", align_bytes=64)

        for k in range(TAPS):
            nc.gpsimd.memset(s_raw[k][:].bitcast(I32), 0)

        def load_dy(a, c):
            nc.sync.dma_start(out=raw[a][c][:], in_=dy_rows[:, a, :, CHUNKS[a][c]:CHUNKS[a][c + 1]])

        def load_list(k):
            nc.sync.dma_start(lists[k][:], lists_in[k])

        def load_words(k):
            nc.sync.dma_start(out=w_raw[k][:].bitcast(I32), in_=words_in[k][0].bitcast(I32))

        def load_scales(k, quadrants):
            for r in quadrants:
                nc.sync.dma_start(
                    out=s_raw[k][32 * r:32 * r + 4, :].bitcast(I32),
                    in_=scales_in[k][0][4 * r:4 * r + 4, :].bitcast(I32),
                )

        load_dy(0, 0)
        load_list(0)
        load_dy(0, 1)
        load_dy(0, 2)
        load_list(1)
        load_list(2)
        load_dy(1, 0)
        load_scales(0, range(1))
        load_dy(1, 1)
        load_scales(0, range(1, 4))
        load_words(0)
        load_scales(1, range(4))
        load_words(1)
        load_scales(2, range(4))
        load_words(2)

        def cast_pairs(a, c, copy):
            copy(
                out=pairs[a][:, 2 * CHUNKS[a][c]:2 * CHUNKS[a][c + 1]].rearrange("p (c i j) -> p c j i", i=RUN, j=2),
                in_=raw[a][c][:].rearrange("p j (c i) -> p c j i", i=RUN),
            )

        rows16 = keep.tile([P, 2 * X], BF16, name="rows16", align_bytes=64)
        for c in range(len(raw[0])):
            cast_pairs(0, c, on_vector)
            nc.scalar.copy(
                out=rows16[:].rearrange("p (j x) -> p j x", j=2)[:, :, CHUNKS[0][c]:CHUNKS[0][c + 1]], in_=raw[0][c][:]
            )
        for c in range(len(raw[1])):
            cast_pairs(1, c, on_scalar)

        def deal(k):
            nc.vector.tensor_copy(
                out=w_dealt[k][:].bitcast(U16).rearrange("p (t m) -> p t m", t=LANES),
                in_=w_raw[k][:].bitcast(U16).rearrange("p (m t) -> p t m", t=LANES),
            )
            nc.vector.tensor_copy(
                out=s_dealt[k][:].rearrange("p (t m) -> p t m", t=LANES),
                in_=s_raw[k][:].rearrange("p (m t) -> p t m", t=LANES),
            )

        acc = [[psum.tile([P, HALF], F32, name="acc%d%d" % (h, t)) for t in range(LANES)] for h in range(2)]

        picked02 = keep.tile([P, 3 * HALF], U32, name="picked02", align_bytes=64)
        picked1 = keep.tile([P, 2 * HALF], U32, name="picked1", tag="picked135", align_bytes=64)
        picked35 = keep.tile([P, 2 * HALF], U32, name="picked35", tag="picked135", align_bytes=64)
        woven2_high = shared.tile([P, LANES * QUARTER], BF16, name="woven2_high", align_bytes=64, offset=WOVEN2_HIGH_AT)
        picked4 = shared.tile([P, 2 * HALF], U32, name="picked4", align_bytes=64, offset=PICKED4_AT)
        picked = [
            picked02[:, HALF:3 * HALF], picked1[:], picked02[:, 0:2 * HALF], picked35[:], picked4[:], picked35[:]
        ]
        woven2_low = picked35[:, HALF:2 * HALF].bitcast(BF16)
        woven = {}
        codes = {}
        scales = {}

        def entries(u):
            h, k = divmod(u, TAPS)
            return lists[k][:, h * HALF // ENTRIES:(h + 1) * HALF // ENTRIES]

        def gather(u, a):
            nc.vector.tensor_copy(
                out=picked[u][:, a * HALF:(a + 1) * HALF], in_=pairs[a][:].bitcast(U32).indirect(entries(u))
            )

        def gather_row(u, j):
            nc.scalar.activation(
                out=picked[u][:, 0:HALF].bitcast(BF16).rearrange("p (x j) -> p j x", j=2)[:, j, :],
                in_=rows16[:, j * X:(j + 1) * X].indirect(entries(u)),
                func=mybir.ActivationFunctionType.Copy,
            )

        def weave(dst, u, lo, hi, copy, word):
            copy(
                out=dst.bitcast(word).rearrange("p (c i a) -> p c a i", i=RUN, a=2),
                in_=picked[u].bitcast(word).rearrange("p (a c i) -> p c a i", a=2, i=RUN)[:, lo // RUN:hi // RUN, :, :],
            )

        def weave_first_half(u):
            woven[u] = ring.tile([P, LANES * HALF], BF16, name="woven", align_bytes=64)
            weave(woven[u][:], u, 0, HALF, on_scalar, U32)

        def weave_second_half(u, offset, copy, word):
            woven[u] = shared.tile([P, LANES * HALF], BF16, name="woven%d" % u, align_bytes=64, offset=offset)
            weave(woven[u][:], u, 0, HALF, copy, word)

        def quantise_columns(u, lo, hi, src):
            nc.vector.quantize_mx(out=codes[u][:, lo:hi].bitcast(E5M2X4), scales=scales[u][:, lo:hi], in_=src)

        def quantise(u):
            codes[u] = ring.tile([P, HALF], U32, name="codes", align_bytes=64)
            scales[u] = ring.tile([P, HALF], U8, name="scales", align_bytes=64)
            quantise_columns(u, 0, HALF, woven[u][:])

        def multiply(u):
            h, k = divmod(u, TAPS)
            for t in range(LANES):
                nc.tensor.matmul_mx(
                    out=acc[h][t][:],
                    lhsT=w_dealt[k][:, 2 * P * t:2 * P * (t + 1)].bitcast(E2M1X4),
                    lhsT_scale=s_dealt[k][:, P * t:P * (t + 1)],
                    rhs=codes[u][:].bitcast(E5M2X4),
                    rhs_scale=scales[u][:],
                    start=(k == 0),
                    stop=(k == TAPS - 1),
                )

        y = [keep.tile([P, LANES, HALF], F32, name="y%d" % h, align_bytes=64) for h in range(2)]
        y16 = [keep.tile([P, LANES * HALF], BF16, name="y16_%d" % h, align_bytes=64) for h in range(2)]

        def empty_bank(h, t, copy):
            copy(out=y[h][:, t, :], in_=acc[h][t][:])
            if t % 2 == 1:
                nc.sync.dma_start(out=out_rows[:, t - 1:t + 1, h * HALF:(h + 1) * HALF], in_=y[h][:, t - 1:t + 1, :])

        def round_result(h, lo, hi, copy):
            copy(
                out=y16[h][:, LANES * lo:LANES * hi].rearrange("p (c i t) -> p c t i", i=RUN, t=LANES),
                in_=y[h][:, :, lo:hi].rearrange("p t (c i) -> p c t i", i=RUN),
            )

        def planes(h, lo, hi):
            cols = slice(h * HALF + lo, h * HALF + hi)
            nc.vector.quantize_mx(
                out=y_codes[:, cols].bitcast(E4M3X4), scales=y_scales[:, cols], in_=y16[h][:, LANES * lo:LANES * hi]
            )
            nc.sync.dma_start(out=out_words[:, cols], in_=y_codes[:, cols].bitcast(I32))

        for u in range(TAPS):
            gather(u, 0)
        deal(0)
        gather(0, 1)
        gather(1, 1)
        weave_first_half(0)
        quantise(0)
        multiply(0)
        gather(2, 1)
        weave_first_half(1)
        gather_row(3, 0)
        quantise(1)
        deal(1)
        multiply(1)
        deal(2)
        weave(woven2_low, 2, 0, QUARTER, on_scalar, U32)
        weave(woven2_high[:], 2, QUARTER, HALF, on_scalar, U32)
        gather_row(3, 1)
        codes[2] = shared.tile([P, HALF], U32, name="codes2", align_bytes=64, offset=CODES2_AT)
        scales[2] = shared.tile([P, HALF], U8, name="scales2", align_bytes=64, offset=SCALES2_AT)
        quantise_columns(2, 0, QUARTER, woven2_low)
        quantise_columns(2, QUARTER, HALF, woven2_high[:])
        multiply(2)

        gather(3, 1)
        gather(4, 0)
        gather(4, 1)
        for t in range(LANES - 1):
            empty_bank(0, t, on_scalar)
        weave_second_half(3, WOVEN3_AT, on_scalar, U32)
        weave_second_half(4, WOVEN4_AT, on_scalar, U32)
        empty_bank(0, LANES - 1, on_scalar)
        quantise(3)
        multiply(3)
        gather(5, 0)
        gather(5, 1)
        quantise(4)
        multiply(4)
        weave_second_half(5, WOVEN5_AT, on_vector, I32)
        quantise(5)
        multiply(5)
        round_result(0, 0, HALF, on_scalar)
        planes(0, 0, HALF)

        for t in range(LANES):
            empty_bank(1, t, on_scalar if t % 2 == 0 else on_vector)
        round_result(1, 0, QUARTER, on_vector)
        round_result(1, QUARTER, VECTOR_COLUMNS, on_vector)
        round_result(1, VECTOR_COLUMNS, HALF, on_scalar)
        planes(1, 0, QUARTER)
        planes(1, QUARTER, HALF)
        for r in range(4):
            queue = nc.sync if r % 2 == 0 else nc.scalar
            queue.dma_start(out=out_scales[4 * r:4 * r + 4, :], in_=y_scales[32 * r:32 * r + 4, :].bitcast(I32))
